import numpy as np
import ml_dtypes


def mxq(x, axis, fmt="e4m3"):
    dtype, down = {"e4m3": (ml_dtypes.float8_e4m3fn, 7), "e5m2": (ml_dtypes.float8_e5m2, 14)}[fmt]
    v = np.moveaxis(np.asarray(x, np.float32).astype(ml_dtypes.bfloat16).astype(np.float64), axis, -1)
    blocks = v.reshape(v.shape[:-1] + (-1, 32))
    amax = np.abs(blocks).max(-1, keepdims=True)
    byte = np.maximum(np.where(amax > 0, np.frexp(amax)[1] - 1 + 127, 0) - down, 1)
    scale = np.exp2(byte - 127.0)
    codes = (blocks / scale).astype(np.float32).astype(dtype).astype(np.float64)
    return np.moveaxis((codes * scale).reshape(v.shape), -1, axis)


WIDE = False


def mx_kscale(k):
    if not WIDE:
        return np.ones(k)
    levels = np.array([10, -10, 5, -5, 0])
    if k % 512:
        return np.exp2(np.random.permutation(np.resize(levels, k // 32))).repeat(32)
    a = np.empty((k // 512, 16))
    for p in range(k // 512):
        a[p, :8] = np.random.permutation(np.resize(levels, 8))
        for g in range(8):
            far = levels[np.abs(levels - a[p, g]) >= 10]
            a[p, g + 8] = far[np.random.randint(len(far))]
    return np.exp2(a.ravel()).repeat(32)


def f64(x):
    return np.asarray(x).astype(np.float64)


def striped(idx):
    return np.tile(idx.reshape(-1, 16).T, (8, 1)).astype(np.uint16)


def unstriped(offs):
    return offs[:16].T.reshape(-1).astype(np.int64)


E2M1 = np.array([0.0, 0.5, 1.0, 1.5, 2.0, 3.0, 4.0, 6.0, -0.0, -0.5, -1.0, -1.5, -2.0, -3.0, -4.0, -6.0])


def pack_weight(w, fmt):
    k, n = w.shape
    w = f64(np.asarray(w, np.float32).astype(ml_dtypes.bfloat16)).reshape(k // 32, 32, n)
    amax = np.abs(w).max(1)
    if fmt == "e4m3":
        byte = np.frexp(amax)[1] - 1 + 127 - 7
    else:
        mant, ex = np.frexp(amax / 6.0)
        byte = np.where(mant > 0.5, ex, ex - 1) + 127
    byte = np.clip(np.where(amax > 0, byte, 1), 1, 254)
    scaled = (w * np.exp2(127.0 - byte)[:, None, :]).reshape(k, n).astype(np.float32)
    by_word = np.ascontiguousarray(scaled.reshape(k // 512, 128, 4, n).transpose(0, 1, 3, 2))
    if fmt == "e4m3":
        words = by_word.astype(ml_dtypes.float8_e4m3fn).view(np.uint8)
    else:
        c = by_word.astype(ml_dtypes.float4_e2m1fn).view(np.uint8) & 0xF
        words = (c[..., 0::2] | (c[..., 1::2] << 4)).reshape(k // 512, 128, 2 * n)
    return np.ascontiguousarray(words), np.ascontiguousarray(byte.astype(np.uint8).reshape(k // 512, 16, n))


def unpack_weight(words, scales, fmt):
    g, _, n = scales.shape
    words = np.ascontiguousarray(words).reshape(g, 128, n, -1)
    if fmt == "e4m3":
        vals = words.view(ml_dtypes.float8_e4m3fn).astype(np.float64)
    else:
        nib = np.empty((g, 128, n, 4), np.uint8)
        nib[..., 0::2] = words & 0xF
        nib[..., 1::2] = words >> 4
        vals = E2M1[nib]
    vals = vals * np.repeat(np.exp2(scales.astype(np.float64) - 127.0), 8, axis=1)[..., None]
    return vals.transpose(0, 1, 3, 2).reshape(g * 512, n)


def gelu(v):
    return 0.5 * v * (1.0 + np.tanh(np.sqrt(2.0 / np.pi) * (v + 0.044715 * v**3)))


def bf(x):
    return np.asarray(x, np.float32).astype(ml_dtypes.bfloat16)

def planes(Y):
    n, m = Y.shape
    b = f64(bf(Y)).reshape(n // 32, 32, m)
    amax = np.abs(b).max(1)
    byte = np.clip(np.where(amax > 0, np.frexp(amax)[1] - 1 + 127 - 7, 1), 1, 254)
    codes = (b * np.exp2(127.0 - byte)[:, None, :]).reshape(n, m).astype(np.float32).astype(ml_dtypes.float8_e4m3fn).view(np.uint8)
    words = codes.reshape(n // 512, 128, 4, m).transpose(0, 1, 3, 2)
    return np.ascontiguousarray(words), np.ascontiguousarray(byte.astype(np.uint8).reshape(n // 512, 16, m))


K, H, N, T, S = 512, 1024, 512, 2048, 1024

def setup_inputs():
    n = np.random.standard_normal
    s = mx_kscale(K)[:, None]
    u = mx_kscale(H)[:, None]
    gain = np.exp(0.8 * n(N))[None, :]
    tab_words, tab_scales = pack_weight(n((K, T)) * s, "e4m3")
    wl_words, wl_scales = pack_weight(n((K, H)) / np.sqrt(K) / s * u.T, "e2m1")
    wr_words, wr_scales = pack_weight(n((K, H)) / np.sqrt(K) / s * u.T, "e4m3")
    wa_words, wa_scales = pack_weight(n((K, N)) / np.sqrt(K) / s * gain, "e4m3")
    wc = n((K, H)) / np.sqrt(K) / s * u.T
    ws = n((H, N)) / np.sqrt(H) / u * gain
    slope0 = (0.6 + 0.4 * np.abs(n(H))) * u[:, 0]
    return {"tab_words": tab_words, "tab_scales": tab_scales,
            "wl_words": wl_words, "wl_scales": wl_scales,
            "wr_words": wr_words, "wr_scales": wr_scales,
            "wa_words": wa_words, "wa_scales": wa_scales,
            "wc": wc.astype(np.float32), "ws": ws.astype(np.float32),
            "slope0": slope0.astype(np.float32),
            "offs": striped(np.random.permutation(T)[:S]),
            "offs2": striped(np.random.permutation(T)[:S]),
            "offs3": striped(np.random.permutation(T)[:S])}

def reference(tab_words, tab_scales, wl_words, wl_scales, wr_words, wr_scales, wa_words, wa_scales,
              wc, ws, slope0, offs, offs2, offs3):
    vl = unpack_weight(tab_words, tab_scales, "e4m3")[:, unstriped(offs)]
    vc = unpack_weight(tab_words, tab_scales, "e4m3")[:, unstriped(offs2)]
    vr = unpack_weight(tab_words, tab_scales, "e4m3")[:, unstriped(offs3)]
    left = unpack_weight(wl_words, wl_scales, "e2m1").T @ vl
    centre = mxq(f64(wc), 0, "e4m3").T @ vc
    right = unpack_weight(wr_words, wr_scales, "e4m3").T @ vr
    h = np.maximum(np.minimum(centre - left, right - centre) + f64(slope0)[:, None], 0.0)
    y = (mxq(f64(ws), 0, "e4m3").T @ mxq(h, 0, "e4m3")
              + unpack_weight(wa_words, wa_scales, "e4m3").T @ vc)
    words, scales = planes(y)
    return y, words, scales

@@ -1,0 +1,306 @@
+from contextlib import ExitStack
+
+import concourse.mybir as mybir
+from concourse.masks import make_identity
+
+K, H, N, T, S = 512, 1024, 512, 2048, 1024
+FLOPS = 2 * S * (3 * K * H + H * N + K * N)
+
+F32 = mybir.dt.float32
+BF16 = mybir.dt.bfloat16
+I32 = mybir.dt.int32
+U32 = mybir.dt.uint32
+U16 = mybir.dt.uint16
+U8 = mybir.dt.uint8
+FP8X4 = mybir.dt.float8_e4m3fn_x4
+FP4X4 = mybir.dt.float4_e2m1fn_x4
+ALU = mybir.AluOpType
+ACT = mybir.ActivationFunctionType
+
+P = 128
+HALF = 512
+QUART = 128
+
+
+def tile_list_limited_reconstruction_kernel(
+    tc, tab_words, tab_scales, wl_words, wl_scales, wr_words, wr_scales, wa_words, wa_scales,
+    wc, ws, slope0, offs, offs2, offs3, out_0, out_1, out_2,
+):
+    nc = tc.nc
+    with ExitStack() as ctx:
+        keep = ctx.enter_context(tc.tile_pool(name="keep", bufs=1))
+        work = ctx.enter_context(tc.tile_pool(name="work", bufs=2))
+        psum = ctx.enter_context(tc.psum_pool(name="psum", bufs=8))
+
+        def held(shape, dtype, name):
+            return keep.tile(shape, dtype, name=name, align_bytes=64)
+
+        def bank():
+            return psum.tile([P, HALF], F32, name="bank")
+
+        slope_rows = held([P, 2 * P], F32, "slope_rows")
+        nc.vector.memset(slope_rows[:], 0.0)
+        w_s_raw = held([P, H], U8, "w_s_raw")
+        nc.gpsimd.memset(w_s_raw[:].bitcast(I32), 0)
+
+        def load_list(name, source):
+            tile = keep.tile([P, S // 16], U16, name="list_" + name)
+            nc.sync.dma_start(tile[:], source)
+            return tile
+
+        def load_plane(queue, plane, scales, width):
+            for q in range(4):
+                row = 32 * q + 4 * plane
+                queue.dma_start(
+                    w_s_raw[row : row + 4, :].bitcast(I32),
+                    scales[0, 4 * q : 4 * q + 4, :].bitcast(I32),
+                )
+
+        lists = {"c": load_list("c", offs2)}
+        tab_s = held([P, T], U8, "tab_s")
+        for q in range(4):
+            nc.sync.dma_start(
+                tab_s[32 * q : 32 * q + 32, :].bitcast(I32),
+                tab_scales[0, 4 * q : 4 * q + 4, :].bitcast(I32).partition_broadcast(8),
+            )
+        wc_raw = [held([P, 4, HALF], F32, "wc_raw%d" % b) for b in range(2)]
+        wc_rows = wc.rearrange("(p j) c -> p j c", j=4)
+        nc.sync.dma_start(wc_raw[0][:], wc_rows[:, :, 0:HALF])
+        nc.sync.dma_start(
+            slope_rows[0:4, :].rearrange("t (g i) -> t g i", i=8),
+            slope0.rearrange("(g t i) -> t g i", t=4, i=8),
+        )
+        lists["l"] = load_list("l", offs)
+        lists["r"] = load_list("r", offs3)
+        nc.sync.dma_start(wc_raw[1][:], wc_rows[:, :, HALF:H])
+        tab_w = held([P, T], U32, "tab_w")
+        nc.sync.dma_start(tab_w[:].bitcast(I32), tab_words[0].rearrange("p n t -> p (n t)").bitcast(I32))
+        wl_raw = held([P, H // 2], I32, "wl_raw")
+        nc.sync.dma_start(wl_raw[:], wl_words[0].bitcast(I32))
+        wr_raw = held([P, H], I32, "wr_raw")
+        nc.sync.dma_start(wr_raw[:], wr_words[0].rearrange("p n t -> p (n t)").bitcast(I32))
+        load_plane(nc.gpsimd, 0, wl_scales, H)
+        load_plane(nc.gpsimd, 1, wr_scales, H)
+        ident = held([P, P], F32, "ident")
+        make_identity(nc, ident[:])
+        ws_raw = [held([P, 4, N], F32, "ws_raw%d" % b) for b in range(2)]
+        ws_rows = ws.rearrange("(b g t i) n -> b t g i n", b=2, t=4, i=8)
+        for b in range(2):
+            for t in range(4):
+                nc.sync.dma_start(ws_raw[b][:, t, :], ws_rows[b, t])
+        wa_raw = held([P, N], I32, "wa_raw")
+        nc.sync.dma_start(wa_raw[:], wa_words[0].rearrange("p n t -> p (n t)").bitcast(I32))
+        wa_s_raw = held([P, N], U8, "wa_s_raw")
+        nc.vector.memset(wa_s_raw[:].bitcast(I32), 0)
+        for q in range(4):
+            nc.sync.dma_start(
+                wa_s_raw[32 * q : 32 * q + 4, :].bitcast(I32),
+                wa_scales[0, 4 * q : 4 * q + 4, :].bitcast(I32),
+            )
+
+        slope_bank = bank()
+        for b in range(2):
+            nc.tensor.transpose(slope_bank[:, P * b : P * b + P], slope_rows[:, P * b : P * b + P], ident[:])
+        slope = held([P, 2, 4], F32, "slope")
+        nc.scalar.activation(
+            slope[:], slope_bank[:, 0 : 2 * P].rearrange("p (b x) -> p b x", b=2)[:, :, 0:4], ACT.Copy
+        )
+
+        v_s, v_w = {}, {}
+        for name in "clr":
+            v_s[name] = held([P, S], U8, "v_s_" + name)
+            nc.vector.tensor_copy(v_s[name][:], tab_s[:].indirect(lists[name][:]))
+        for name in "clr":
+            v_w[name] = held([P, S], U32, "v_w_" + name)
+
+        def gather_words(name, h):
+            nc.vector.tensor_copy(
+                v_w[name][:, HALF * h : HALF * h + HALF],
+                tab_w[:].indirect(lists[name][:, 32 * h : 32 * h + 32]),
+            )
+
+        for name in "clr":
+            gather_words(name, 0)
+
+        wc_w = held([P, H], U32, "wc_w")
+        wc_s = held([P, H], U8, "wc_s")
+        ws_w = held([P, 2 * N], U32, "ws_w")
+        ws_s = held([P, 2 * N], U8, "ws_s")
+
+        def quantise(words, scales, values):
+            nc.vector.quantize_mx(out=words.bitcast(FP8X4), scales=scales, in_=values)
+
+        def prepare_wc(b):
+            rounded = work.tile([P, 4 * HALF], BF16, name="w_rounded", align_bytes=64)
+            dst = rounded[:].rearrange("p (t g i j) -> p t g j i", t=4, i=8, j=4)
+            src = wc_raw[b][:].rearrange("p j (g t i) -> p t g j i", t=4, i=8)
+            for t in range(4):
+                nc.scalar.activation(dst[:, t], src[:, t], ACT.Copy, scale=-1.0)
+            cols = slice(HALF * b, HALF * b + HALF)
+            quantise(wc_w[:, cols], wc_s[:, cols], rounded[:])
+
+        def prepare_ws(b):
+            rounded = work.tile([P, 4 * N], BF16, name="w_rounded", align_bytes=64)
+            dst = rounded[:].rearrange("p (t m j) -> p m j t", t=4, j=4)
+            src = ws_raw[b][:].rearrange("p j (m t) -> p m j t", t=4)
+            for m0 in range(0, P, 64):
+                nc.scalar.activation(dst[:, m0 : m0 + 64], src[:, m0 : m0 + 64], ACT.Copy)
+            cols = slice(N * b, N * b + N)
+            quantise(ws_w[:, cols], ws_s[:, cols], rounded[:])
+
+        def deal_runs(dst, src, run):
+            nc.vector.tensor_copy(
+                dst.rearrange("p (b t g i) -> p b t g i", b=2, t=4, i=run),
+                src.rearrange("p (b g t i) -> p b t g i", b=2, t=4, i=run),
+            )
+
+        prepare_wc(0)
+        wl_w = held([P, 2 * H], U8, "wl_w")
+        deal_runs(wl_w[:].bitcast(I32), wl_raw[:], 4)
+        wr_w = held([P, H], U32, "wr_w")
+        deal_runs(wr_w[:].bitcast(I32), wr_raw[:], 8)
+        wlr_s = held([P, H], U8, "wlr_s")
+        deal_runs(wlr_s[:].bitcast(I32), w_s_raw[:].bitcast(I32), 2)
+        prepare_wc(1)
+        for name in "clr":
+            gather_words(name, 1)
+        wa_w = held([P, N], U32, "wa_w")
+        nc.vector.tensor_copy(
+            wa_w[:].bitcast(I32).rearrange("p (t o i) -> p o t i", t=4, i=4),
+            wa_raw[:].rearrange("p (o i t) -> p o t i", t=4, i=4),
+        )
+        wa_s = held([P, N], U8, "wa_s")
+        nc.vector.tensor_copy(
+            wa_s[:].rearrange("p (t m) -> p t m", t=4),
+            wa_s_raw[:].rearrange("p (m t) -> p t m", t=4),
+        )
+        prepare_ws(0)
+        prepare_ws(1)
+
+        def first_pass(out, name, b, t, h, start, stop):
+            c0 = HALF * b + P * t
+            cols = slice(c0, c0 + P)
+            if name == "c":
+                words, scales = wc_w[:, cols].bitcast(FP8X4), wc_s[:, cols]
+            elif name == "l":
+                words, scales = wl_w[:, 2 * c0 : 2 * c0 + 2 * P].bitcast(FP4X4), wlr_s[:, cols]
+            else:
+                words, scales = wr_w[:, cols].bitcast(FP8X4), wlr_s[4:P, cols]
+            toks = slice(HALF * h, HALF * h + HALF)
+            nc.tensor.matmul_mx(
+                out, lhsT=words, lhsT_scale=scales,
+                rhs=v_w[name][:, toks].bitcast(FP8X4), rhs_scale=v_s[name][:, toks],
+                start=start, stop=stop,
+            )
+
+        def slope_tile(m, h, b, t):
+            s = slope[:, b, t : t + 1]
+            index = 8 * h + 4 * b + t
+            staged = ws_raw[1 - b][:, t, :]
+            if index % 2 == 1 and index > 1:
+                lc, rc = bank(), bank()
+                first_pass(lc[:], "c", b, t, h, True, False)
+                first_pass(lc[:], "l", b, t, h, False, True)
+                first_pass(rc[:], "c", b, t, h, True, False)
+                first_pass(rc[:], "r", b, t, h, False, True)
+                nc.scalar.activation(staged, lc[:], ACT.Identity, bias=s, scale=-1.0)
+                nc.vector.scalar_tensor_tensor(m[:, t, :], rc[:], s, staged, ALU.add, ALU.min)
+            else:
+                c, l, r = bank(), bank(), bank()
+                first_pass(c[:], "c", b, t, h, True, True)
+                first_pass(l[:], "l", b, t, h, True, True)
+                first_pass(r[:], "r", b, t, h, True, True)
+                nc.scalar.activation(staged, c[:], ACT.Copy, scale=-1.0)
+                sides = work.tile([P, 2, HALF], BF16, name="sides", bufs=2)
+                nc.vector.scalar_tensor_tensor(sides[:, 0, :], staged, s, l[:], ALU.add, ALU.subtract)
+                nc.vector.scalar_tensor_tensor(sides[:, 1, :], r[:], s, staged, ALU.add, ALU.subtract)
+                nc.vector.tensor_tensor(m[:, t, :], sides[:, 0, :], sides[:, 1, :], ALU.min)
+
+        h_w = [[held([P, HALF], U32, "h_w%d%d" % (h, b)) for b in range(2)] for h in range(2)]
+        h_s = [[held([P, HALF], U8, "h_s%d%d" % (h, b)) for b in range(2)] for h in range(2)]
+
+        def cut_and_weave(dst, m, j0, j1, on_vector):
+            out = dst.rearrange("p (o i t) -> p o t i", t=4, i=4)
+            src = m[:, :, j0:j1].rearrange("p t (o i) -> p o t i", i=4)
+            if on_vector:
+                nc.vector.tensor_scalar(out, src, 0.0, None, ALU.max)
+            else:
+                nc.scalar.activation(out, src, ACT.Relu)
+
+        def quantise_h(m, h, b):
+            woven = work.tile([P, 4 * HALF], BF16, name="woven", align_bytes=64)
+            last = h == 1 and b == 1
+            for q in range(4):
+                on_vector = last and q % 2 == 0
+                cut_and_weave(woven[:, HALF * q : HALF * q + HALF], m, QUART * q, QUART * q + QUART, on_vector)
+                if last:
+                    cols = slice(QUART * q, QUART * q + QUART)
+                    quantise(h_w[h][b][:, cols], h_s[h][b][:, cols], woven[:, HALF * q : HALF * q + HALF])
+            if not last:
+                quantise(h_w[h][b][:], h_s[h][b][:], woven[:])
+
+        y_w = held([P, S], U32, "y_w")
+        y_s = held([P, S], U8, "y_s")
+        out_rows = out_0.rearrange("(p t) j -> p t j", t=4)
+        out_words = out_1[0].rearrange("p m t -> p (m t)").bitcast(I32)
+
+        def second_pass(out, part, t, h, q, start, stop):
+            cols = slice(P * t, P * t + P)
+            toks = slice(QUART * q, QUART * q + QUART)
+            if part == 2:
+                words, scales = wa_w[:, cols], wa_s[:, cols]
+                j0 = HALF * h + QUART * q
+                mov_w, mov_s = v_w["c"][:, j0 : j0 + QUART], v_s["c"][:, j0 : j0 + QUART]
+            else:
+                c0 = N * part + P * t
+                words, scales = ws_w[:, c0 : c0 + P], ws_s[:, c0 : c0 + P]
+                mov_w, mov_s = h_w[h][part][:, toks], h_s[h][part][:, toks]
+            nc.tensor.matmul_mx(
+                out[:, cols], lhsT=words.bitcast(FP8X4), lhsT_scale=scales,
+                rhs=mov_w.bitcast(FP8X4), rhs_scale=mov_s, start=start, stop=stop,
+            )
+
+        def face_state(h):
+            last = h == 1
+            order = (2, 0, 1) if last else (1, 0, 2)
+            y_woven = work.tile([P, 4 * HALF], BF16, name="y_woven", align_bytes=64)
+            for q in range(4):
+                acc = bank()
+                for n, part in enumerate(order):
+                    for t in range(4):
+                        second_pass(acc, part, t, h, q, n == 0 and t == 0, n == 2 and t == 3)
+                y = work.tile([P, 4, QUART], F32, name="y", bufs=8)
+                nc.scalar.copy(y[:], acc[:].rearrange("p (t j) -> p t j", t=4))
+                cols = slice(HALF * h + QUART * q, HALF * h + QUART * q + QUART)
+                nc.sync.dma_start(out_rows[:, :, cols], y[:])
+                dst = y_woven[:, HALF * q : HALF * q + HALF]
+                if last:
+                    nc.vector.tensor_copy(
+                        dst.rearrange("p (o i t) -> p o t i", t=4, i=4),
+                        y[:].rearrange("p t (o i) -> p o t i", i=4),
+                    )
+                    quantise(y_w[:, cols], y_s[:, cols], dst)
+                    nc.sync.dma_start(out_words[:, cols], y_w[:, cols].bitcast(I32))
+                else:
+                    nc.scalar.copy(
+                        dst.rearrange("p (j t) -> p j t", t=4), acc[:].rearrange("p (t j) -> p j t", t=4)
+                    )
+            if not last:
+                cols = slice(HALF * h, HALF * h + HALF)
+                quantise(y_w[:, cols], y_s[:, cols], y_woven[:])
+                nc.sync.dma_start(out_words[:, cols], y_w[:, cols].bitcast(I32))
+
+        for h in range(2):
+            for b in range(2):
+                m = work.tile([P, 4, HALF], BF16, name="m", bufs=2)
+                for t in range(4):
+                    slope_tile(m, h, b, t)
+                    if (h, b, t) == (1, 0, 1):
+                        face_state(0)
+                quantise_h(m, h, b)
+        face_state(1)
+        for q in range(4):
+            nc.scalar.dma_start(
+                out_2[0, 4 * q : 4 * q + 4, :].bitcast(I32),
+                y_s[32 * q : 32 * q + 4, :].bitcast(I32),
+            )

@@ -19,7 +19,8 @@ ACT = mybir.ActivationFunctionType
 
 P = 128
 HALF = 512
-QUART = 128
+CHUNK = 128
+PLAIN = (2, 2, 3, 2)
 
 
 def tile_list_limited_reconstruction_kernel(
@@ -41,7 +42,9 @@ def tile_list_limited_reconstruction_kernel(
         slope_rows = held([P, 2 * P], F32, "slope_rows")
         nc.vector.memset(slope_rows[:], 0.0)
         w_s_raw = held([P, H], U8, "w_s_raw")
-        nc.gpsimd.memset(w_s_raw[:].bitcast(I32), 0)
+        nc.vector.memset(w_s_raw[:].bitcast(I32), 0)
+        ident = held([P, P], F32, "ident")
+        make_identity(nc, ident[:])
 
         def load_list(name, source):
             tile = keep.tile([P, S // 16], U16, name="list_" + name)
@@ -59,7 +62,7 @@ def tile_list_limited_reconstruction_kernel(
         lists = {"c": load_list("c", offs2)}
         tab_s = held([P, T], U8, "tab_s")
         for q in range(4):
-            nc.sync.dma_start(
+            (nc.sync if q < 2 else nc.scalar).dma_start(
                 tab_s[32 * q : 32 * q + 32, :].bitcast(I32),
                 tab_scales[0, 4 * q : 4 * q + 4, :].bitcast(I32).partition_broadcast(8),
             )
@@ -72,22 +75,21 @@ def tile_list_limited_reconstruction_kernel(
         )
         lists["l"] = load_list("l", offs)
         lists["r"] = load_list("r", offs3)
-        nc.sync.dma_start(wc_raw[1][:], wc_rows[:, :, HALF:H])
         tab_w = held([P, T], U32, "tab_w")
         nc.sync.dma_start(tab_w[:].bitcast(I32), tab_words[0].rearrange("p n t -> p (n t)").bitcast(I32))
+        nc.sync.dma_start(wc_raw[1][:], wc_rows[:, :, HALF:H])
+        ws_raw = [held([P, 4, N], F32, "ws_raw%d" % b) for b in range(2)]
+        ws_rows = ws.rearrange("(b g t i) n -> b t g i n", b=2, t=4, i=8)
+        for t in range(4):
+            nc.sync.dma_start(ws_raw[0][:, t, :], ws_rows[0, t])
+        load_plane(nc.sync, 0, wl_scales, H)
         wl_raw = held([P, H // 2], I32, "wl_raw")
         nc.sync.dma_start(wl_raw[:], wl_words[0].bitcast(I32))
         wr_raw = held([P, H], I32, "wr_raw")
         nc.sync.dma_start(wr_raw[:], wr_words[0].rearrange("p n t -> p (n t)").bitcast(I32))
-        load_plane(nc.gpsimd, 0, wl_scales, H)
-        load_plane(nc.gpsimd, 1, wr_scales, H)
-        ident = held([P, P], F32, "ident")
-        make_identity(nc, ident[:])
-        ws_raw = [held([P, 4, N], F32, "ws_raw%d" % b) for b in range(2)]
-        ws_rows = ws.rearrange("(b g t i) n -> b t g i n", b=2, t=4, i=8)
-        for b in range(2):
-            for t in range(4):
-                nc.sync.dma_start(ws_raw[b][:, t, :], ws_rows[b, t])
+        load_plane(nc.sync, 1, wr_scales, H)
+        for t in range(4):
+            nc.sync.dma_start(ws_raw[1][:, t, :], ws_rows[1, t])
         wa_raw = held([P, N], I32, "wa_raw")
         nc.sync.dma_start(wa_raw[:], wa_words[0].rearrange("p n t -> p (n t)").bitcast(I32))
         wa_s_raw = held([P, N], U8, "wa_s_raw")
@@ -112,15 +114,7 @@ def tile_list_limited_reconstruction_kernel(
             nc.vector.tensor_copy(v_s[name][:], tab_s[:].indirect(lists[name][:]))
         for name in "clr":
             v_w[name] = held([P, S], U32, "v_w_" + name)
-
-        def gather_words(name, h):
-            nc.vector.tensor_copy(
-                v_w[name][:, HALF * h : HALF * h + HALF],
-                tab_w[:].indirect(lists[name][:, 32 * h : 32 * h + 32]),
-            )
-
-        for name in "clr":
-            gather_words(name, 0)
+            nc.vector.tensor_copy(v_w[name][:], tab_w[:].indirect(lists[name][:]))
 
         wc_w = held([P, H], U32, "wc_w")
         wc_s = held([P, H], U8, "wc_s")
@@ -130,23 +124,18 @@ def tile_list_limited_reconstruction_kernel(
         def quantise(words, scales, values):
             nc.vector.quantize_mx(out=words.bitcast(FP8X4), scales=scales, in_=values)
 
-        def prepare_wc(b):
-            rounded = work.tile([P, 4 * HALF], BF16, name="w_rounded", align_bytes=64)
-            dst = rounded[:].rearrange("p (t g i j) -> p t g j i", t=4, i=8, j=4)
+        wc_rounded = held([P, 4 * H], BF16, "wc_rounded")
+        for b in range(2):
+            dst = wc_rounded[:, 4 * HALF * b : 4 * HALF * (b + 1)].rearrange("p (t g i j) -> p t g j i", t=4, i=8, j=4)
             src = wc_raw[b][:].rearrange("p j (g t i) -> p t g j i", t=4, i=8)
             for t in range(4):
                 nc.scalar.activation(dst[:, t], src[:, t], ACT.Copy, scale=-1.0)
-            cols = slice(HALF * b, HALF * b + HALF)
-            quantise(wc_w[:, cols], wc_s[:, cols], rounded[:])
-
-        def prepare_ws(b):
-            rounded = work.tile([P, 4 * N], BF16, name="w_rounded", align_bytes=64)
-            dst = rounded[:].rearrange("p (t m j) -> p m j t", t=4, j=4)
-            src = ws_raw[b][:].rearrange("p j (m t) -> p m j t", t=4)
-            for m0 in range(0, P, 64):
-                nc.scalar.activation(dst[:, m0 : m0 + 64], src[:, m0 : m0 + 64], ACT.Copy)
-            cols = slice(N * b, N * b + N)
-            quantise(ws_w[:, cols], ws_s[:, cols], rounded[:])
+        ws_rounded = held([P, 8 * N], BF16, "ws_rounded")
+        for b in range(2):
+            nc.scalar.copy(
+                ws_rounded[:, 4 * N * b : 4 * N * (b + 1)].rearrange("p (t m j) -> p m j t", t=4, j=4),
+                ws_raw[b][:].rearrange("p j (m t) -> p m j t", t=4),
+            )
 
         def deal_runs(dst, src, run):
             nc.vector.tensor_copy(
@@ -154,28 +143,24 @@ def tile_list_limited_reconstruction_kernel(
                 src.rearrange("p (b g t i) -> p b t g i", b=2, t=4, i=run),
             )
 
-        prepare_wc(0)
+        quantise(wc_w[:], wc_s[:], wc_rounded[:])
         wl_w = held([P, 2 * H], U8, "wl_w")
         deal_runs(wl_w[:].bitcast(I32), wl_raw[:], 4)
         wr_w = held([P, H], U32, "wr_w")
         deal_runs(wr_w[:].bitcast(I32), wr_raw[:], 8)
         wlr_s = held([P, H], U8, "wlr_s")
         deal_runs(wlr_s[:].bitcast(I32), w_s_raw[:].bitcast(I32), 2)
-        prepare_wc(1)
-        for name in "clr":
-            gather_words(name, 1)
         wa_w = held([P, N], U32, "wa_w")
+        wa_s = held([P, N], U8, "wa_s")
         nc.vector.tensor_copy(
             wa_w[:].bitcast(I32).rearrange("p (t o i) -> p o t i", t=4, i=4),
             wa_raw[:].rearrange("p (o i t) -> p o t i", t=4, i=4),
         )
-        wa_s = held([P, N], U8, "wa_s")
         nc.vector.tensor_copy(
             wa_s[:].rearrange("p (t m) -> p t m", t=4),
             wa_s_raw[:].rearrange("p (m t) -> p t m", t=4),
         )
-        prepare_ws(0)
-        prepare_ws(1)
+        quantise(ws_w[:], ws_s[:], ws_rounded[:])
 
         def first_pass(out, name, b, t, h, start, stop):
             c0 = HALF * b + P * t
@@ -193,11 +178,10 @@ def tile_list_limited_reconstruction_kernel(
                 start=start, stop=stop,
             )
 
-        def slope_tile(m, h, b, t):
+        def slope_tile(m, sides, h, b, t):
             s = slope[:, b, t : t + 1]
-            index = 8 * h + 4 * b + t
             staged = ws_raw[1 - b][:, t, :]
-            if index % 2 == 1 and index > 1:
+            if t >= PLAIN[2 * h + b]:
                 lc, rc = bank(), bank()
                 first_pass(lc[:], "c", b, t, h, True, False)
                 first_pass(lc[:], "l", b, t, h, False, True)
@@ -211,10 +195,8 @@ def tile_list_limited_reconstruction_kernel(
                 first_pass(l[:], "l", b, t, h, True, True)
                 first_pass(r[:], "r", b, t, h, True, True)
                 nc.scalar.activation(staged, c[:], ACT.Copy, scale=-1.0)
-                sides = work.tile([P, 2, HALF], BF16, name="sides", bufs=2)
-                nc.vector.scalar_tensor_tensor(sides[:, 0, :], staged, s, l[:], ALU.add, ALU.subtract)
-                nc.vector.scalar_tensor_tensor(sides[:, 1, :], r[:], s, staged, ALU.add, ALU.subtract)
-                nc.vector.tensor_tensor(m[:, t, :], sides[:, 0, :], sides[:, 1, :], ALU.min)
+                nc.vector.scalar_tensor_tensor(sides[0][:, t, :], staged, s, l[:], ALU.add, ALU.subtract)
+                nc.vector.scalar_tensor_tensor(sides[1][:, t, :], r[:], s, staged, ALU.add, ALU.subtract)
 
         h_w = [[held([P, HALF], U32, "h_w%d%d" % (h, b)) for b in range(2)] for h in range(2)]
         h_s = [[held([P, HALF], U8, "h_s%d%d" % (h, b)) for b in range(2)] for h in range(2)]
@@ -227,80 +209,99 @@ def tile_list_limited_reconstruction_kernel(
             else:
                 nc.scalar.activation(out, src, ACT.Relu)
 
-        def quantise_h(m, h, b):
-            woven = work.tile([P, 4 * HALF], BF16, name="woven", align_bytes=64)
-            last = h == 1 and b == 1
-            for q in range(4):
-                on_vector = last and q % 2 == 0
-                cut_and_weave(woven[:, HALF * q : HALF * q + HALF], m, QUART * q, QUART * q + QUART, on_vector)
-                if last:
-                    cols = slice(QUART * q, QUART * q + QUART)
-                    quantise(h_w[h][b][:, cols], h_s[h][b][:, cols], woven[:, HALF * q : HALF * q + HALF])
-            if not last:
-                quantise(h_w[h][b][:], h_s[h][b][:], woven[:])
-
         y_w = held([P, S], U32, "y_w")
         y_s = held([P, S], U8, "y_s")
         out_rows = out_0.rearrange("(p t) j -> p t j", t=4)
         out_words = out_1[0].rearrange("p m t -> p (m t)").bitcast(I32)
 
-        def second_pass(out, part, t, h, q, start, stop):
-            cols = slice(P * t, P * t + P)
-            toks = slice(QUART * q, QUART * q + QUART)
+        def second_pass(out, part, t, h, c, start, stop):
+            toks = slice(CHUNK * c, CHUNK * c + CHUNK)
             if part == 2:
-                words, scales = wa_w[:, cols], wa_s[:, cols]
-                j0 = HALF * h + QUART * q
-                mov_w, mov_s = v_w["c"][:, j0 : j0 + QUART], v_s["c"][:, j0 : j0 + QUART]
+                words, scales = wa_w[:, P * t : P * t + P], wa_s[:, P * t : P * t + P]
+                j0 = HALF * h + CHUNK * c
+                mov_w, mov_s = v_w["c"][:, j0 : j0 + CHUNK], v_s["c"][:, j0 : j0 + CHUNK]
             else:
                 c0 = N * part + P * t
                 words, scales = ws_w[:, c0 : c0 + P], ws_s[:, c0 : c0 + P]
                 mov_w, mov_s = h_w[h][part][:, toks], h_s[h][part][:, toks]
             nc.tensor.matmul_mx(
-                out[:, cols], lhsT=words.bitcast(FP8X4), lhsT_scale=scales,
+                out, lhsT=words.bitcast(FP8X4), lhsT_scale=scales,
                 rhs=mov_w.bitcast(FP8X4), rhs_scale=mov_s, start=start, stop=stop,
             )
 
-        def face_state(h):
-            last = h == 1
-            order = (2, 0, 1) if last else (1, 0, 2)
-            y_woven = work.tile([P, 4 * HALF], BF16, name="y_woven", align_bytes=64)
-            for q in range(4):
-                acc = bank()
-                for n, part in enumerate(order):
-                    for t in range(4):
-                        second_pass(acc, part, t, h, q, n == 0 and t == 0, n == 2 and t == 3)
-                y = work.tile([P, 4, QUART], F32, name="y", bufs=8)
-                nc.scalar.copy(y[:], acc[:].rearrange("p (t j) -> p t j", t=4))
-                cols = slice(HALF * h + QUART * q, HALF * h + QUART * q + QUART)
-                nc.sync.dma_start(out_rows[:, :, cols], y[:])
-                dst = y_woven[:, HALF * q : HALF * q + HALF]
-                if last:
-                    nc.vector.tensor_copy(
-                        dst.rearrange("p (o i t) -> p o t i", t=4, i=4),
-                        y[:].rearrange("p t (o i) -> p o t i", i=4),
-                    )
-                    quantise(y_w[:, cols], y_s[:, cols], dst)
-                    nc.sync.dma_start(out_words[:, cols], y_w[:, cols].bitcast(I32))
-                else:
-                    nc.scalar.copy(
-                        dst.rearrange("p (j t) -> p j t", t=4), acc[:].rearrange("p (t j) -> p j t", t=4)
-                    )
-            if not last:
-                cols = slice(HALF * h, HALF * h + HALF)
-                quantise(y_w[:, cols], y_s[:, cols], y_woven[:])
-                nc.sync.dma_start(out_words[:, cols], y_w[:, cols].bitcast(I32))
+        y = [[held([P, 4, CHUNK], F32, "y%d%d" % (h, c)) for c in range(4)] for h in range(2)]
+        y_woven = [held([P, 4 * HALF], BF16, "y_woven%d" % h) for h in range(2)]
 
-        for h in range(2):
-            for b in range(2):
-                m = work.tile([P, 4, HALF], BF16, name="m", bufs=2)
+        def woven_part(tile, c0, c1):
+            return tile[:, 4 * CHUNK * c0 : 4 * CHUNK * c1]
+
+        def face_state(h, c, order, weave_first):
+            acc = bank()
+            for n, part in enumerate(order):
                 for t in range(4):
-                    slope_tile(m, h, b, t)
-                    if (h, b, t) == (1, 0, 1):
-                        face_state(0)
-                quantise_h(m, h, b)
-        face_state(1)
+                    second_pass(acc[:, CHUNK * t : CHUNK * t + CHUNK], part, t, h, c,
+                                n == 0 and t == 0, n == 2 and t == 3)
+            if weave_first:
+                nc.vector.tensor_copy(
+                    woven_part(y_woven[h], c, c + 1).rearrange("p (j t) -> p j t", t=4),
+                    acc[:].rearrange("p (t j) -> p j t", t=4),
+                )
+            nc.scalar.copy(y[h][c][:], acc[:].rearrange("p (t j) -> p t j", t=4))
+            cols = slice(HALF * h + CHUNK * c, HALF * h + CHUNK * c + CHUNK)
+            nc.sync.dma_start(out_rows[:, :, cols], y[h][c][:])
+
+        def weave_y(h, c):
+            nc.vector.tensor_copy(
+                woven_part(y_woven[h], c, c + 1).rearrange("p (o i t) -> p o t i", t=4, i=4),
+                y[h][c][:].rearrange("p t (o i) -> p o t i", i=4),
+            )
+
+        def store_planes(h, c0, c1):
+            cols = slice(HALF * h + CHUNK * c0, HALF * h + CHUNK * c1)
+            quantise(y_w[:, cols], y_s[:, cols], woven_part(y_woven[h], c0, c1))
+            nc.sync.dma_start(out_words[:, cols], y_w[:, cols].bitcast(I32))
+
+        slopes = [held([P, 4, HALF], BF16, "slopes%d" % g) for g in range(4)]
+        woven = [held([P, 4 * HALF], BF16, "woven%d" % g) for g in range(4)]
+
+        def weave(g, c0, c1, on_vector):
+            cut_and_weave(woven_part(woven[g], c0, c1), slopes[g], CHUNK * c0, CHUNK * c1, on_vector)
+
+        for g in range(4):
+            h, b = divmod(g, 2)
+            m = slopes[g]
+            sides = [work.tile([P, 3, HALF], BF16, name="side%d" % n) for n in range(2)]
+            for t in range(4):
+                slope_tile(m, sides, h, b, t)
+                if t == PLAIN[g]:
+                    nc.vector.tensor_tensor(m[:, 0:t, :], sides[0][:, 0:t, :], sides[1][:, 0:t, :], ALU.min)
+                if g > 0 and t < 2:
+                    weave(g - 1, 2 * t, 2 * t + 2, False)
+                if g > 0 and t == 2:
+                    quantise(h_w[(g - 1) // 2][(g - 1) % 2][:], h_s[(g - 1) // 2][(g - 1) % 2][:], woven[g - 1][:])
+                piece = 4 * g + t - 11
+                if 0 <= piece < 4:
+                    face_state(0, piece, (1, 0, 2), False)
+                if 1 <= piece < 3:
+                    weave_y(0, piece - 1)
+                if piece == 3:
+                    store_planes(0, 0, 2)
+        for c in range(4):
+            weave(3, c, c + 1, c % 2 == 0)
+            cols = slice(CHUNK * c, CHUNK * c + CHUNK)
+            quantise(h_w[1][1][:, cols], h_s[1][1][:, cols], woven_part(woven[3], c, c + 1))
+        weave_y(0, 2)
+        weave_y(0, 3)
+        store_planes(0, 2, 4)
+        for c in range(4):
+            face_state(1, c, (2, 0, 1), c == 3)
+        weave_y(1, 0)
+        weave_y(1, 1)
+        store_planes(1, 0, 2)
+        weave_y(1, 2)
+        store_planes(1, 2, 4)
         for q in range(4):
-            nc.scalar.dma_start(
+            (nc.scalar if q < 3 else nc.sync).dma_start(
                 out_2[0, 4 * q : 4 * q + 4, :].bitcast(I32),
                 y_s[32 * q : 32 * q + 4, :].bitcast(I32),
             )

@@ -20,6 +20,7 @@ ACT = mybir.ActivationFunctionType
 P = 128
 HALF = 512
 CHUNK = 128
+F32_MAX = 3.4028234663852886e38
 PLAIN = (2, 2, 3, 2)
 
 
@@ -242,7 +243,7 @@ def tile_list_limited_reconstruction_kernel(
                     second_pass(acc[:, CHUNK * t : CHUNK * t + CHUNK], part, t, h, c,
                                 n == 0 and t == 0, n == 2 and t == 3)
             if weave_first:
-                nc.vector.tensor_copy(
+                weave_first(
                     woven_part(y_woven[h], c, c + 1).rearrange("p (j t) -> p j t", t=4),
                     acc[:].rearrange("p (t j) -> p j t", t=4),
                 )
@@ -276,14 +277,16 @@ def tile_list_limited_reconstruction_kernel(
                 if t == PLAIN[g]:
                     nc.vector.tensor_tensor(m[:, 0:t, :], sides[0][:, 0:t, :], sides[1][:, 0:t, :], ALU.min)
                 if g > 0 and t < 2:
-                    weave(g - 1, 2 * t, 2 * t + 2, False)
+                    nc.gpsimd.tensor_scalar(
+                        woven_part(woven[g - 1], 2 * t, 2 * t + 2).rearrange("p (j t) -> p j t", t=4),
+                        slopes[g - 1][:, :, 2 * CHUNK * t : 2 * CHUNK * (t + 1)].rearrange("p t j -> p j t"),
+                        F32_MAX, 0.0, ALU.min, ALU.max,
+                    )
                 if g > 0 and t == 2:
                     quantise(h_w[(g - 1) // 2][(g - 1) % 2][:], h_s[(g - 1) // 2][(g - 1) % 2][:], woven[g - 1][:])
                 piece = 4 * g + t - 11
                 if 0 <= piece < 4:
-                    face_state(0, piece, (1, 0, 2), False)
-                if 1 <= piece < 3:
-                    weave_y(0, piece - 1)
+                    face_state(0, piece, (1, 0, 2), nc.scalar.copy if piece < 2 else None)
                 if piece == 3:
                     store_planes(0, 0, 2)
         for c in range(4):
@@ -294,7 +297,7 @@ def tile_list_limited_reconstruction_kernel(
         weave_y(0, 3)
         store_planes(0, 2, 4)
         for c in range(4):
-            face_state(1, c, (2, 0, 1), c == 3)
+            face_state(1, c, (2, 0, 1), nc.vector.tensor_copy if c == 3 else None)
         weave_y(1, 0)
         weave_y(1, 1)
         store_planes(1, 0, 2)

from contextlib import ExitStack

import concourse.mybir as mybir
from concourse.masks import make_identity

K, H, N, T, S = 512, 1024, 512, 2048, 1024
FLOPS = 2 * S * (3 * K * H + H * N + K * N)

F32 = mybir.dt.float32
BF16 = mybir.dt.bfloat16
I32 = mybir.dt.int32
U32 = mybir.dt.uint32
U16 = mybir.dt.uint16
U8 = mybir.dt.uint8
FP8X4 = mybir.dt.float8_e4m3fn_x4
FP4X4 = mybir.dt.float4_e2m1fn_x4
ALU = mybir.AluOpType
ACT = mybir.ActivationFunctionType

P = 128
HALF = 512
CHUNK = 128
F32_MAX = 3.4028234663852886e38
PLAIN = (2, 2, 3, 2)


def tile_list_limited_reconstruction_kernel(
    tc, tab_words, tab_scales, wl_words, wl_scales, wr_words, wr_scales, wa_words, wa_scales,
    wc, ws, slope0, offs, offs2, offs3, out_0, out_1, out_2,
):
    nc = tc.nc
    with ExitStack() as ctx:
        keep = ctx.enter_context(tc.tile_pool(name="keep", bufs=1))
        work = ctx.enter_context(tc.tile_pool(name="work", bufs=2))
        psum = ctx.enter_context(tc.psum_pool(name="psum", bufs=8))

        def held(shape, dtype, name):
            return keep.tile(shape, dtype, name=name, align_bytes=64)

        def bank():
            return psum.tile([P, HALF], F32, name="bank")

        slope_rows = held([P, 2 * P], F32, "slope_rows")
        nc.vector.memset(slope_rows[:], 0.0)
        w_s_raw = held([P, H], U8, "w_s_raw")
        nc.vector.memset(w_s_raw[:].bitcast(I32), 0)
        ident = held([P, P], F32, "ident")
        make_identity(nc, ident[:])

        def load_list(name, source):
            tile = keep.tile([P, S // 16], U16, name="list_" + name)
            nc.sync.dma_start(tile[:], source)
            return tile

        def load_plane(queue, plane, scales, width):
            for q in range(4):
                row = 32 * q + 4 * plane
                queue.dma_start(
                    w_s_raw[row : row + 4, :].bitcast(I32),
                    scales[0, 4 * q : 4 * q + 4, :].bitcast(I32),
                )

        lists = {"c": load_list("c", offs2)}
        tab_s = held([P, T], U8, "tab_s")
        for q in range(4):
            (nc.sync if q < 2 else nc.scalar).dma_start(
                tab_s[32 * q : 32 * q + 32, :].bitcast(I32),
                tab_scales[0, 4 * q : 4 * q + 4, :].bitcast(I32).partition_broadcast(8),
            )
        wc_raw = [held([P, 4, HALF], F32, "wc_raw%d" % b) for b in range(2)]
        wc_rows = wc.rearrange("(p j) c -> p j c", j=4)
        nc.sync.dma_start(wc_raw[0][:], wc_rows[:, :, 0:HALF])
        nc.sync.dma_start(
            slope_rows[0:4, :].rearrange("t (g i) -> t g i", i=8),
            slope0.rearrange("(g t i) -> t g i", t=4, i=8),
        )
        lists["l"] = load_list("l", offs)
        lists["r"] = load_list("r", offs3)
        tab_w = held([P, T], U32, "tab_w")
        nc.sync.dma_start(tab_w[:].bitcast(I32), tab_words[0].rearrange("p n t -> p (n t)").bitcast(I32))
        nc.sync.dma_start(wc_raw[1][:], wc_rows[:, :, HALF:H])
        ws_raw = [held([P, 4, N], F32, "ws_raw%d" % b) for b in range(2)]
        ws_rows = ws.rearrange("(b g t i) n -> b t g i n", b=2, t=4, i=8)
        for t in range(4):
            nc.sync.dma_start(ws_raw[0][:, t, :], ws_rows[0, t])
        load_plane(nc.sync, 0, wl_scales, H)
        wl_raw = held([P, H // 2], I32, "wl_raw")
        nc.sync.dma_start(wl_raw[:], wl_words[0].bitcast(I32))
        wr_raw = held([P, H], I32, "wr_raw")
        nc.sync.dma_start(wr_raw[:], wr_words[0].rearrange("p n t -> p (n t)").bitcast(I32))
        load_plane(nc.sync, 1, wr_scales, H)
        for t in range(4):
            nc.sync.dma_start(ws_raw[1][:, t, :], ws_rows[1, t])
        wa_raw = held([P, N], I32, "wa_raw")
        nc.sync.dma_start(wa_raw[:], wa_words[0].rearrange("p n t -> p (n t)").bitcast(I32))
        wa_s_raw = held([P, N], U8, "wa_s_raw")
        nc.vector.memset(wa_s_raw[:].bitcast(I32), 0)
        for q in range(4):
            nc.sync.dma_start(
                wa_s_raw[32 * q : 32 * q + 4, :].bitcast(I32),
                wa_scales[0, 4 * q : 4 * q + 4, :].bitcast(I32),
            )

        slope_bank = bank()
        for b in range(2):
            nc.tensor.transpose(slope_bank[:, P * b : P * b + P], slope_rows[:, P * b : P * b + P], ident[:])
        slope = held([P, 2, 4], F32, "slope")
        nc.scalar.activation(
            slope[:], slope_bank[:, 0 : 2 * P].rearrange("p (b x) -> p b x", b=2)[:, :, 0:4], ACT.Copy
        )

        v_s, v_w = {}, {}
        for name in "clr":
            v_s[name] = held([P, S], U8, "v_s_" + name)
            nc.vector.tensor_copy(v_s[name][:], tab_s[:].indirect(lists[name][:]))
        for name in "clr":
            v_w[name] = held([P, S], U32, "v_w_" + name)
            nc.vector.tensor_copy(v_w[name][:], tab_w[:].indirect(lists[name][:]))

        wc_w = held([P, H], U32, "wc_w")
        wc_s = held([P, H], U8, "wc_s")
        ws_w = held([P, 2 * N], U32, "ws_w")
        ws_s = held([P, 2 * N], U8, "ws_s")

        def quantise(words, scales, values):
            nc.vector.quantize_mx(out=words.bitcast(FP8X4), scales=scales, in_=values)

        wc_rounded = held([P, 4 * H], BF16, "wc_rounded")
        for b in range(2):
            dst = wc_rounded[:, 4 * HALF * b : 4 * HALF * (b + 1)].rearrange("p (t g i j) -> p t g j i", t=4, i=8, j=4)
            src = wc_raw[b][:].rearrange("p j (g t i) -> p t g j i", t=4, i=8)
            for t in range(4):
                nc.scalar.activation(dst[:, t], src[:, t], ACT.Copy, scale=-1.0)
        ws_rounded = held([P, 8 * N], BF16, "ws_rounded")
        for b in range(2):
            nc.scalar.copy(
                ws_rounded[:, 4 * N * b : 4 * N * (b + 1)].rearrange("p (t m j) -> p m j t", t=4, j=4),
                ws_raw[b][:].rearrange("p j (m t) -> p m j t", t=4),
            )

        def deal_runs(dst, src, run):
            nc.vector.tensor_copy(
                dst.rearrange("p (b t g i) -> p b t g i", b=2, t=4, i=run),
                src.rearrange("p (b g t i) -> p b t g i", b=2, t=4, i=run),
            )

        quantise(wc_w[:], wc_s[:], wc_rounded[:])
        wl_w = held([P, 2 * H], U8, "wl_w")
        deal_runs(wl_w[:].bitcast(I32), wl_raw[:], 4)
        wr_w = held([P, H], U32, "wr_w")
        deal_runs(wr_w[:].bitcast(I32), wr_raw[:], 8)
        wlr_s = held([P, H], U8, "wlr_s")
        deal_runs(wlr_s[:].bitcast(I32), w_s_raw[:].bitcast(I32), 2)
        wa_w = held([P, N], U32, "wa_w")
        wa_s = held([P, N], U8, "wa_s")
        nc.vector.tensor_copy(
            wa_w[:].bitcast(I32).rearrange("p (t o i) -> p o t i", t=4, i=4),
            wa_raw[:].rearrange("p (o i t) -> p o t i", t=4, i=4),
        )
        nc.vector.tensor_copy(
            wa_s[:].rearrange("p (t m) -> p t m", t=4),
            wa_s_raw[:].rearrange("p (m t) -> p t m", t=4),
        )
        quantise(ws_w[:], ws_s[:], ws_rounded[:])

        def first_pass(out, name, b, t, h, start, stop):
            c0 = HALF * b + P * t
            cols = slice(c0, c0 + P)
            if name == "c":
                words, scales = wc_w[:, cols].bitcast(FP8X4), wc_s[:, cols]
            elif name == "l":
                words, scales = wl_w[:, 2 * c0 : 2 * c0 + 2 * P].bitcast(FP4X4), wlr_s[:, cols]
            else:
                words, scales = wr_w[:, cols].bitcast(FP8X4), wlr_s[4:P, cols]
            toks = slice(HALF * h, HALF * h + HALF)
            nc.tensor.matmul_mx(
                out, lhsT=words, lhsT_scale=scales,
                rhs=v_w[name][:, toks].bitcast(FP8X4), rhs_scale=v_s[name][:, toks],
                start=start, stop=stop,
            )

        def slope_tile(m, sides, h, b, t):
            s = slope[:, b, t : t + 1]
            staged = ws_raw[1 - b][:, t, :]
            if t >= PLAIN[2 * h + b]:
                lc, rc = bank(), bank()
                first_pass(lc[:], "c", b, t, h, True, False)
                first_pass(lc[:], "l", b, t, h, False, True)
                first_pass(rc[:], "c", b, t, h, True, False)
                first_pass(rc[:], "r", b, t, h, False, True)
                nc.scalar.activation(staged, lc[:], ACT.Identity, bias=s, scale=-1.0)
                nc.vector.scalar_tensor_tensor(m[:, t, :], rc[:], s, staged, ALU.add, ALU.min)
            else:
                c, l, r = bank(), bank(), bank()
                first_pass(c[:], "c", b, t, h, True, True)
                first_pass(l[:], "l", b, t, h, True, True)
                first_pass(r[:], "r", b, t, h, True, True)
                nc.scalar.activation(staged, c[:], ACT.Copy, scale=-1.0)
                nc.vector.scalar_tensor_tensor(sides[0][:, t, :], staged, s, l[:], ALU.add, ALU.subtract)
                nc.vector.scalar_tensor_tensor(sides[1][:, t, :], r[:], s, staged, ALU.add, ALU.subtract)

        h_w = [[held([P, HALF], U32, "h_w%d%d" % (h, b)) for b in range(2)] for h in range(2)]
        h_s = [[held([P, HALF], U8, "h_s%d%d" % (h, b)) for b in range(2)] for h in range(2)]

        def cut_and_weave(dst, m, j0, j1, on_vector):
            out = dst.rearrange("p (o i t) -> p o t i", t=4, i=4)
            src = m[:, :, j0:j1].rearrange("p t (o i) -> p o t i", i=4)
            if on_vector:
                nc.vector.tensor_scalar(out, src, 0.0, None, ALU.max)
            else:
                nc.scalar.activation(out, src, ACT.Relu)

        y_w = held([P, S], U32, "y_w")
        y_s = held([P, S], U8, "y_s")
        out_rows = out_0.rearrange("(p t) j -> p t j", t=4)
        out_words = out_1[0].rearrange("p m t -> p (m t)").bitcast(I32)

        def second_pass(out, part, t, h, c, start, stop):
            toks = slice(CHUNK * c, CHUNK * c + CHUNK)
            if part == 2:
                words, scales = wa_w[:, P * t : P * t + P], wa_s[:, P * t : P * t + P]
                j0 = HALF * h + CHUNK * c
                mov_w, mov_s = v_w["c"][:, j0 : j0 + CHUNK], v_s["c"][:, j0 : j0 + CHUNK]
            else:
                c0 = N * part + P * t
                words, scales = ws_w[:, c0 : c0 + P], ws_s[:, c0 : c0 + P]
                mov_w, mov_s = h_w[h][part][:, toks], h_s[h][part][:, toks]
            nc.tensor.matmul_mx(
                out, lhsT=words.bitcast(FP8X4), lhsT_scale=scales,
                rhs=mov_w.bitcast(FP8X4), rhs_scale=mov_s, start=start, stop=stop,
            )

        y = [[held([P, 4, CHUNK], F32, "y%d%d" % (h, c)) for c in range(4)] for h in range(2)]
        y_woven = [held([P, 4 * HALF], BF16, "y_woven%d" % h) for h in range(2)]

        def woven_part(tile, c0, c1):
            return tile[:, 4 * CHUNK * c0 : 4 * CHUNK * c1]

        def face_state(h, c, order, weave_first):
            acc = bank()
            for n, part in enumerate(order):
                for t in range(4):
                    second_pass(acc[:, CHUNK * t : CHUNK * t + CHUNK], part, t, h, c,
                                n == 0 and t == 0, n == 2 and t == 3)
            if weave_first:
                weave_first(
                    woven_part(y_woven[h], c, c + 1).rearrange("p (j t) -> p j t", t=4),
                    acc[:].rearrange("p (t j) -> p j t", t=4),
                )
            nc.scalar.copy(y[h][c][:], acc[:].rearrange("p (t j) -> p t j", t=4))
            cols = slice(HALF * h + CHUNK * c, HALF * h + CHUNK * c + CHUNK)
            nc.sync.dma_start(out_rows[:, :, cols], y[h][c][:])

        def weave_y(h, c):
            nc.vector.tensor_copy(
                woven_part(y_woven[h], c, c + 1).rearrange("p (o i t) -> p o t i", t=4, i=4),
                y[h][c][:].rearrange("p t (o i) -> p o t i", i=4),
            )

        def store_planes(h, c0, c1):
            cols = slice(HALF * h + CHUNK * c0, HALF * h + CHUNK * c1)
            quantise(y_w[:, cols], y_s[:, cols], woven_part(y_woven[h], c0, c1))
            nc.sync.dma_start(out_words[:, cols], y_w[:, cols].bitcast(I32))

        slopes = [held([P, 4, HALF], BF16, "slopes%d" % g) for g in range(4)]
        woven = [held([P, 4 * HALF], BF16, "woven%d" % g) for g in range(4)]

        def weave(g, c0, c1, on_vector):
            cut_and_weave(woven_part(woven[g], c0, c1), slopes[g], CHUNK * c0, CHUNK * c1, on_vector)

        for g in range(4):
            h, b = divmod(g, 2)
            m = slopes[g]
            sides = [work.tile([P, 3, HALF], BF16, name="side%d" % n) for n in range(2)]
            for t in range(4):
                slope_tile(m, sides, h, b, t)
                if t == PLAIN[g]:
                    nc.vector.tensor_tensor(m[:, 0:t, :], sides[0][:, 0:t, :], sides[1][:, 0:t, :], ALU.min)
                if g > 0 and t < 2:
                    nc.gpsimd.tensor_scalar(
                        woven_part(woven[g - 1], 2 * t, 2 * t + 2).rearrange("p (j t) -> p j t", t=4),
                        slopes[g - 1][:, :, 2 * CHUNK * t : 2 * CHUNK * (t + 1)].rearrange("p t j -> p j t"),
                        F32_MAX, 0.0, ALU.min, ALU.max,
                    )
                if g > 0 and t == 2:
                    quantise(h_w[(g - 1) // 2][(g - 1) % 2][:], h_s[(g - 1) // 2][(g - 1) % 2][:], woven[g - 1][:])
                piece = 4 * g + t - 11
                if 0 <= piece < 4:
                    face_state(0, piece, (1, 0, 2), nc.scalar.copy if piece < 2 else None)
                if piece == 3:
                    store_planes(0, 0, 2)
        for c in range(4):
            weave(3, c, c + 1, c % 2 == 0)
            cols = slice(CHUNK * c, CHUNK * c + CHUNK)
            quantise(h_w[1][1][:, cols], h_s[1][1][:, cols], woven_part(woven[3], c, c + 1))
        weave_y(0, 2)
        weave_y(0, 3)
        store_planes(0, 2, 4)
        for c in range(4):
            face_state(1, c, (2, 0, 1), nc.vector.tensor_copy if c == 3 else None)
        weave_y(1, 0)
        weave_y(1, 1)
        store_planes(1, 0, 2)
        weave_y(1, 2)
        store_planes(1, 2, 4)
        for q in range(4):
            (nc.scalar if q < 3 else nc.sync).dma_start(
                out_2[0, 4 * q : 4 * q + 4, :].bitcast(I32),
                y_s[32 * q : 32 * q + 4, :].bitcast(I32),
            )
